import numpy as np
import ml_dtypes


def mxq(x, axis, fmt="e4m3"):
    dtype, down = {"e4m3": (ml_dtypes.float8_e4m3fn, 7), "e5m2": (ml_dtypes.float8_e5m2, 14)}[fmt]
    v = np.moveaxis(np.asarray(x, np.float32).astype(ml_dtypes.bfloat16).astype(np.float64), axis, -1)
    blocks = v.reshape(v.shape[:-1] + (-1, 32))
    amax = np.abs(blocks).max(-1, keepdims=True)
    byte = np.maximum(np.where(amax > 0, np.frexp(amax)[1] - 1 + 127, 0) - down, 1)
    scale = np.exp2(byte - 127.0)
    codes = (blocks / scale).astype(np.float32).astype(dtype).astype(np.float64)
    return np.moveaxis((codes * scale).reshape(v.shape), -1, axis)


WIDE = False


def mx_kscale(k):
    if not WIDE:
        return np.ones(k)
    levels = np.array([10, -10, 5, -5, 0])
    if k % 512:
        return np.exp2(np.random.permutation(np.resize(levels, k // 32))).repeat(32)
    a = np.empty((k // 512, 16))
    for p in range(k // 512):
        a[p, :8] = np.random.permutation(np.resize(levels, 8))
        for g in range(8):
            far = levels[np.abs(levels - a[p, g]) >= 10]
            a[p, g + 8] = far[np.random.randint(len(far))]
    return np.exp2(a.ravel()).repeat(32)


def f64(x):
    return np.asarray(x).astype(np.float64)


def striped(idx):
    return np.tile(idx.reshape(-1, 16).T, (8, 1)).astype(np.uint16)


def unstriped(offs):
    return offs[:16].T.reshape(-1).astype(np.int64)


E2M1 = np.array([0.0, 0.5, 1.0, 1.5, 2.0, 3.0, 4.0, 6.0, -0.0, -0.5, -1.0, -1.5, -2.0, -3.0, -4.0, -6.0])


def pack_weight(w, fmt):
    k, n = w.shape
    w = f64(np.asarray(w, np.float32).astype(ml_dtypes.bfloat16)).reshape(k // 32, 32, n)
    amax = np.abs(w).max(1)
    if fmt == "e4m3":
        byte = np.frexp(amax)[1] - 1 + 127 - 7
    else:
        mant, ex = np.frexp(amax / 6.0)
        byte = np.where(mant > 0.5, ex, ex - 1) + 127
    byte = np.clip(np.where(amax > 0, byte, 1), 1, 254)
    scaled = (w * np.exp2(127.0 - byte)[:, None, :]).reshape(k, n).astype(np.float32)
    by_word = np.ascontiguousarray(scaled.reshape(k // 512, 128, 4, n).transpose(0, 1, 3, 2))
    if fmt == "e4m3":
        words = by_word.astype(ml_dtypes.float8_e4m3fn).view(np.uint8)
    else:
        c = by_word.astype(ml_dtypes.float4_e2m1fn).view(np.uint8) & 0xF
        words = (c[..., 0::2] | (c[..., 1::2] << 4)).reshape(k // 512, 128, 2 * n)
    return np.ascontiguousarray(words), np.ascontiguousarray(byte.astype(np.uint8).reshape(k // 512, 16, n))


def unpack_weight(words, scales, fmt):
    g, _, n = scales.shape
    words = np.ascontiguousarray(words).reshape(g, 128, n, -1)
    if fmt == "e4m3":
        vals = words.view(ml_dtypes.float8_e4m3fn).astype(np.float64)
    else:
        nib = np.empty((g, 128, n, 4), np.uint8)
        nib[..., 0::2] = words & 0xF
        nib[..., 1::2] = words >> 4
        vals = E2M1[nib]
    vals = vals * np.repeat(np.exp2(scales.astype(np.float64) - 127.0), 8, axis=1)[..., None]
    return vals.transpose(0, 1, 3, 2).reshape(g * 512, n)


def silu(v):
    return v / (1.0 + np.exp(-np.maximum(v, -700.0)))


K, T, E, C, H, N = 1536, 1280, 4, 256, 512, 384


def by_expert(wq, xq):
    return np.concatenate([wq[e].T @ xq[:, e * C:(e + 1) * C] for e in range(E)], axis=1)


def setup_inputs():
    n = np.random.standard_normal
    s = mx_kscale(K)[:, None]
    u = mx_kscale(H)
    x = pack_weight(n((K, T)) * s, "e4m3")
    return {
        "x_words": x[0],
        "x_scales": x[1],
        "xr": n((N, T)).astype(np.float32),
        "w1": (n((E, K, H)) / np.sqrt(K) / s[None]).astype(np.float32),
        "w3": (n((E, K, H)) / np.sqrt(K) / s[None] * u[None, None, :]).astype(np.float32),
        "w2": (n((E, H, N)) / np.sqrt(H) / u[None, :, None]).astype(np.float32),
        "gate": np.tile(np.random.uniform(0.2, 1.0, E * C), (N, 1)).astype(np.float32),
        "offs": striped(np.random.permutation(T)[:E * C]),
    }


def reference(x_words, x_scales, xr, w1, w3, w2, gate, offs):
    idx = unstriped(offs)
    xq = unpack_weight(x_words, x_scales, "e4m3")[:, idx]
    h = silu(by_expert(mxq(f64(w1), 1, "e4m3"), xq))
    h = h * by_expert(mxq(f64(w3), 1, "e4m3"), xq)
    y = by_expert(mxq(f64(w2), 1, "e4m3"), mxq(h, 0, "e4m3"))
    out = f64(xr).copy()
    out[:, idx] += f64(gate) * y
    return out

@@ -1,0 +1,223 @@
+from contextlib import ExitStack
+
+import concourse.mybir as mybir
+from concourse.masks import make_identity
+
+K, T, E, C, H, N = 1536, 1280, 4, 256, 512, 384
+S = E * C
+FLOPS = 2 * S * (2 * K * H + H * N)
+BYTES = K * T + K * T // 32 + 4 * (2 * N * T + E * (2 * K * H + H * N) + S) + 2 * 8 * S
+
+F32 = mybir.dt.float32
+BF16 = mybir.dt.bfloat16
+I32 = mybir.dt.int32
+U32 = mybir.dt.uint32
+U16 = mybir.dt.uint16
+U8 = mybir.dt.uint8
+FP8X4 = mybir.dt.float8_e4m3fn_x4
+MULT = mybir.AluOpType.mult
+ADD = mybir.AluOpType.add
+SILU = mybir.ActivationFunctionType.Silu
+
+P = 128
+PACK = 4
+K_PASS = P * PACK
+PASSES = K // K_PASS
+N_BLOCKS = N // P
+SLOT_TILES = C // P
+GATHER = 512
+PER_COL = 16
+RAW_BUFS = 10
+
+
+def tile_moe_res_glu_silu_kernel(
+    tc, x_words, x_scales, xr, w1, w3, w2, gate, offs, out
+):
+    nc = tc.nc
+    with ExitStack() as ctx:
+        keep = ctx.enter_context(tc.tile_pool(name="keep", bufs=1))
+        raws = ctx.enter_context(tc.tile_pool(name="raws", bufs=RAW_BUFS))
+        halves = ctx.enter_context(tc.tile_pool(name="halves", bufs=10))
+        coded = ctx.enter_context(tc.tile_pool(name="coded", bufs=8))
+        work = ctx.enter_context(tc.tile_pool(name="work", bufs=2))
+        results = ctx.enter_context(tc.tile_pool(name="results", bufs=3))
+        psum = ctx.enter_context(tc.psum_pool(name="psum", bufs=1))
+
+        offsets = keep.tile([P, S // PER_COL], U16, name="offsets")
+        nc.sync.dma_start(offsets[:], offs)
+
+        token_scales = keep.tile([P, T], U8, name="token_scales", align_bytes=64)
+        nc.vector.memset(token_scales[:].bitcast(I32), 0)
+        windows = [keep.tile([P, T], F32, name=f"window{b}") for b in range(N_BLOCKS)]
+        nc.vector.memset(windows[0][:], 0.0)
+        for window in windows[1:]:
+            nc.gpsimd.memset(window[:], 0.0)
+        identity = keep.tile([P, P], F32, name="identity")
+        make_identity(nc, identity[:])
+        warm = keep.tile([P, 1], F32, name="warm")
+        nc.scalar.activation(warm[:], windows[0][:, 0:1], SILU)
+
+        token_words = [keep.tile([P, T], U32, name=f"token_words{o}", align_bytes=64) for o in range(PASSES)]
+        slot_words = [keep.tile([P, S], U32, name=f"slot_words{o}", align_bytes=64) for o in range(PASSES)]
+        slot_scales = keep.tile([P, S], U8, name="slot_scales", align_bytes=64)
+        gates = keep.tile([P, S], F32, name="gates")
+
+        def load_tokens(o):
+            nc.sync.dma_start(
+                token_words[o][:].bitcast(I32), x_words[o].rearrange("p t r -> p (t r)").bitcast(I32)
+            )
+
+        def load_token_scales(q):
+            nc.sync.dma_start(
+                token_scales[:].bitcast(I32)[32 * q : 32 * q + PACK * PASSES, :],
+                x_scales.bitcast(I32)[:, PACK * q : PACK * (q + 1), :],
+            )
+
+        def gather(s0):
+            listed = offsets[:, s0 // PER_COL : (s0 + GATHER) // PER_COL]
+            for dst, src in list(zip(slot_words, token_words)) + [(slot_scales, token_scales)]:
+                nc.vector.tensor_copy(dst[:, s0 : s0 + GATHER], src[:].indirect(listed))
+
+        def load_rows(rows):
+            raw = raws.tile([P, PACK, rows.shape[1]], F32, name="raw", tag="raw")
+            nc.sync.dma_start(raw[:], rows.rearrange("(p j) w -> p j w", j=PACK))
+            return raw
+
+        def operand_tiles(width):
+            half = halves.tile([P, PACK * width], BF16, name="half", tag="half", align_bytes=64)
+            codes = coded.tile([P, width], U32, name="codes", tag="codes", align_bytes=64)
+            scales = coded.tile([P, width], U8, name="scales", tag="scales", align_bytes=64)
+            return half, codes, scales
+
+        def round_rows(copy, half, c0, raw):
+            c1 = c0 + raw.shape[2]
+            copy(
+                half[:, PACK * c0 : PACK * c1].rearrange("p (c i j) -> p c j i", i=4, j=PACK),
+                raw[:].rearrange("p j (c i) -> p c j i", i=4),
+            )
+
+        def quantise(half, codes, scales, c0, c1):
+            nc.vector.quantize_mx(
+                out=codes[:, c0:c1].bitcast(FP8X4), scales=scales[:, c0:c1], in_=half[:, PACK * c0 : PACK * c1]
+            )
+
+        def multiply_pass(e, o, banks, codes, scales):
+            for st in range(SLOT_TILES):
+                slots = slice(e * C + st * P, e * C + (st + 1) * P)
+                nc.tensor.matmul_mx(
+                    out=banks[st][:],
+                    lhsT=slot_words[o][:, slots].bitcast(FP8X4),
+                    lhsT_scale=slot_scales[PACK * o : P, slots],
+                    rhs=codes[:].bitcast(FP8X4),
+                    rhs_scale=scales[:],
+                    start=(o == 0),
+                    stop=(o == PASSES - 1),
+                )
+
+        def by_word(bank):
+            return bank[:].rearrange("s (p u r) -> s u p r", u=2, r=2)
+
+        def scatter(e, b, sums, y):
+            listed = offsets[:, e * C // PER_COL : (e + 1) * C // PER_COL]
+            nc.scalar.copy(y, sums[b])
+            nc.vector.tensor_tensor(windows[b][:].indirect(listed), y, gates[:, e * C : (e + 1) * C], MULT)
+
+        head = []
+        for o in range(PASSES):
+            load_tokens(o)
+            head.append(load_rows(w1[0, o * K_PASS : (o + 1) * K_PASS, :]))
+            load_token_scales(o)
+            if o == 0:
+                load_token_scales(PASSES)
+
+        residual = []
+        sums = None
+        for e in range(E):
+            last = e == E - 1
+            if e * C % GATHER == 0:
+                gather(e * C)
+            a_banks = [psum.tile([P, H], F32, name=f"a{st}", tag=f"a{st}") for st in range(SLOT_TILES)]
+            b_banks = [psum.tile([P, H], F32, name=f"b{st}", tag=f"b{st}") for st in range(SLOT_TILES)]
+            for step in range(2 * PASSES):
+                o = step % PASSES
+                weights, banks = ((w1, a_banks), (w3, b_banks))[step // PASSES]
+                rows = weights[e, o * K_PASS : (o + 1) * K_PASS, :]
+                half, codes, scales = operand_tiles(H)
+                if last and step == 2 * PASSES - 1:
+                    for copy, c0 in ((nc.scalar.copy, 0), (nc.vector.tensor_copy, H // 2)):
+                        raw = load_rows(rows[:, c0 : c0 + H // 2])
+                        round_rows(copy, half, c0, raw)
+                        quantise(half, codes, scales, c0, c0 + H // 2)
+                else:
+                    raw = head[o] if e == 0 and step < PASSES else load_rows(rows)
+                    round_rows(nc.vector.tensor_copy if o == 0 else nc.scalar.copy, half, 0, raw)
+                    quantise(half, codes, scales, 0, H)
+                multiply_pass(e, o, banks, codes, scales)
+                if e > 0:
+                    if step == 0:
+                        scatter(e - 1, 0, sums, raw[:, 0, 0:C])
+                    if step == 2 and not last:
+                        scatter(e - 1, 1, sums, raw[:, 0, 0:C])
+                    if step == 3 and not last:
+                        scatter(e - 1, 2, sums, raw[:, 0, 0:C])
+                    if step == 4 and last:
+                        scatter(e - 1, 1, sums, half[:, 0 : 2 * C].bitcast(F32))
+                if step == 4:
+                    acts = [raw[:, st, :].rearrange("s (u p r) -> s u p r", u=2, r=2) for st in range(SLOT_TILES)]
+                    for st in range(SLOT_TILES):
+                        nc.scalar.activation(acts[st], by_word(a_banks[st]), SILU)
+            w2_raw = load_rows(w2[e])
+            if e == 0:
+                nc.sync.dma_start(gates[:], gate[0:P, :])
+            if last:
+                for b in range(N_BLOCKS):
+                    rows = raws.tile([P, T], F32, name="rows", tag="raw")
+                    nc.sync.dma_start(rows[:], xr[b * P : (b + 1) * P, :])
+                    residual.append(rows)
+
+            hidden_t = work.tile([P, C * PACK], BF16, name="hidden_t", align_bytes=64)
+            for st in range(SLOT_TILES):
+                hidden = work.tile([P, H], BF16, name="hidden", tag=f"hidden{st}")
+                nc.vector.tensor_tensor(
+                    hidden[:].rearrange("s (u p r) -> s u p r", u=2, r=2), by_word(b_banks[st]), acts[st], MULT
+                )
+                turned = psum.tile([P, 2, P], F32, name="turned", tag=f"turned{st}")
+                for u in range(2):
+                    nc.tensor.transpose(turned[:, u, :], hidden[:].bitcast(F32)[:, u * P : (u + 1) * P], identity[:])
+                nc.scalar.copy(
+                    hidden_t[:].bitcast(F32)[:, st * 2 * P : (st + 1) * 2 * P].rearrange("p (s u) -> p s u", u=2),
+                    turned[:].rearrange("p u s -> p s u"),
+                )
+            h_codes = work.tile([P, C], U32, name="h_codes", align_bytes=64)
+            h_scales = work.tile([P, C], U8, name="h_scales", align_bytes=64)
+            nc.vector.quantize_mx(out=h_codes[:].bitcast(FP8X4), scales=h_scales[:], in_=hidden_t[:])
+
+            half, w2_codes, w2_scales = operand_tiles(N)
+            round_rows(nc.scalar.copy, half, 0, w2_raw)
+            quantise(half, w2_codes, w2_scales, 0, 256)
+            quantise(half, w2_codes, w2_scales, 256, N)
+            if last:
+                scatter(e - 1, 2, sums, hidden[:].bitcast(F32))
+            y_first = psum.tile([P, C], F32, name="y_first")
+            y_rest = psum.tile([P, N_BLOCKS - 1, C], F32, name="y_rest")
+            sums = [y_first[:]] + [y_rest[:, b, :] for b in range(N_BLOCKS - 1)]
+            for b in range(N_BLOCKS):
+                cols = slice(b * P, (b + 1) * P)
+                nc.tensor.matmul_mx(
+                    out=sums[b],
+                    lhsT=w2_codes[:, cols].bitcast(FP8X4),
+                    lhsT_scale=w2_scales[:, cols],
+                    rhs=h_codes[:].bitcast(FP8X4),
+                    rhs_scale=h_scales[:],
+                    start=True,
+                    stop=True,
+                )
+
+        for b in range(N_BLOCKS):
+            y = results.tile([P, C], F32, name="y")
+            scatter(E - 1, b, sums, y[:])
+            pieces = 2 if b == N_BLOCKS - 1 else 1
+            for piece in range(pieces):
+                cols = slice(piece * T // pieces, (piece + 1) * T // pieces)
+                nc.vector.tensor_tensor(residual[b][:, cols], residual[b][:, cols], windows[b][:, cols], ADD)
+                nc.sync.dma_start(out[b * P : (b + 1) * P, cols], residual[b][:, cols])

@@ -93,7 +93,7 @@ def tile_moe_res_glu_silu_kernel(
             c1 = c0 + raw.shape[2]
             copy(
                 half[:, PACK * c0 : PACK * c1].rearrange("p (c i j) -> p c j i", i=4, j=PACK),
-                raw[:].rearrange("p j (c i) -> p c j i", i=4),
+                raw.rearrange("p j (c i) -> p c j i", i=4),
             )
 
         def quantise(half, codes, scales, c0, c1):
@@ -146,23 +146,19 @@ def tile_moe_res_glu_silu_kernel(
                 if last and step == 2 * PASSES - 1:
                     for copy, c0 in ((nc.scalar.copy, 0), (nc.vector.tensor_copy, H // 2)):
                         raw = load_rows(rows[:, c0 : c0 + H // 2])
-                        round_rows(copy, half, c0, raw)
+                        round_rows(copy, half, c0, raw[:])
                         quantise(half, codes, scales, c0, c0 + H // 2)
                 else:
                     raw = head[o] if e == 0 and step < PASSES else load_rows(rows)
-                    round_rows(nc.vector.tensor_copy if o == 0 else nc.scalar.copy, half, 0, raw)
+                    round_rows(nc.vector.tensor_copy if step < 2 else nc.scalar.copy, half, 0, raw[:])
                     quantise(half, codes, scales, 0, H)
                 multiply_pass(e, o, banks, codes, scales)
-                if e > 0:
-                    if step == 0:
-                        scatter(e - 1, 0, sums, raw[:, 0, 0:C])
-                    if step == 2 and not last:
-                        scatter(e - 1, 1, sums, raw[:, 0, 0:C])
-                    if step == 3 and not last:
-                        scatter(e - 1, 2, sums, raw[:, 0, 0:C])
-                    if step == 4 and last:
-                        scatter(e - 1, 1, sums, half[:, 0 : 2 * C].bitcast(F32))
-                if step == 4:
+                if e > 0 and step == 3:
+                    for b in range(N_BLOCKS - 1 if last else N_BLOCKS):
+                        scatter(e - 1, b, sums, raw[:, b, 0:C])
+                if last and step == 4:
+                    scatter(e - 1, N_BLOCKS - 1, sums, half[:, 0 : 2 * C].bitcast(F32))
+                if step == (4 if last else 5):
                     acts = [raw[:, st, :].rearrange("s (u p r) -> s u p r", u=2, r=2) for st in range(SLOT_TILES)]
                     for st in range(SLOT_TILES):
                         nc.scalar.activation(acts[st], by_word(a_banks[st]), SILU)
@@ -184,7 +180,7 @@ def tile_moe_res_glu_silu_kernel(
                 turned = psum.tile([P, 2, P], F32, name="turned", tag=f"turned{st}")
                 for u in range(2):
                     nc.tensor.transpose(turned[:, u, :], hidden[:].bitcast(F32)[:, u * P : (u + 1) * P], identity[:])
-                nc.scalar.copy(
+                (nc.scalar.copy if last else nc.vector.tensor_copy)(
                     hidden_t[:].bitcast(F32)[:, st * 2 * P : (st + 1) * 2 * P].rearrange("p (s u) -> p s u", u=2),
                     turned[:].rearrange("p u s -> p s u"),
                 )
@@ -193,11 +189,13 @@ def tile_moe_res_glu_silu_kernel(
             nc.vector.quantize_mx(out=h_codes[:].bitcast(FP8X4), scales=h_scales[:], in_=hidden_t[:])
 
             half, w2_codes, w2_scales = operand_tiles(N)
-            round_rows(nc.scalar.copy, half, 0, w2_raw)
+            if last:
+                round_rows(nc.scalar.copy, half, 0, w2_raw[:])
+            else:
+                round_rows(nc.vector.tensor_copy, half, 0, w2_raw[:, :, 0 : N // 2])
+                round_rows(nc.scalar.copy, half, N // 2, w2_raw[:, :, N // 2 : N])
             quantise(half, w2_codes, w2_scales, 0, 256)
             quantise(half, w2_codes, w2_scales, 256, N)
-            if last:
-                scatter(e - 1, 2, sums, hidden[:].bitcast(F32))
             y_first = psum.tile([P, C], F32, name="y_first")
             y_rest = psum.tile([P, N_BLOCKS - 1, C], F32, name="y_rest")
             sums = [y_first[:]] + [y_rest[:, b, :] for b in range(N_BLOCKS - 1)]

@@ -122,6 +122,19 @@ def tile_moe_res_glu_silu_kernel(
             nc.scalar.copy(y, sums[b])
             nc.vector.tensor_tensor(windows[b][:].indirect(listed), y, gates[:, e * C : (e + 1) * C], MULT)
 
+        per_row = S // P
+        gate_cols = keep.tile([P, per_row], F32, name="gate_cols")
+        nc.sync.dma_start(gate_cols[:], gate[0:1, :].rearrange("o (p m) -> (o p) m", m=per_row))
+        for g in range(per_row // 4):
+            spread = psum.tile([P, 4, P], F32, name="spread", tag=f"a{g}")
+            for m in range(4):
+                column = gate_cols[:, 4 * g + m : 4 * g + m + 1].to_broadcast([P, P])
+                nc.tensor.transpose(spread[:, m, :], column, identity[:])
+            nc.scalar.copy(
+                gates[:].rearrange("q (p m) -> q p m", m=per_row)[:, :, 4 * g : 4 * g + 4],
+                spread[:].rearrange("q m p -> q p m"),
+            )
+
         head = []
         for o in range(PASSES):
             load_tokens(o)
@@ -150,7 +163,11 @@ def tile_moe_res_glu_silu_kernel(
                         quantise(half, codes, scales, c0, c0 + H // 2)
                 else:
                     raw = head[o] if e == 0 and step < PASSES else load_rows(rows)
-                    round_rows(nc.vector.tensor_copy if step < 2 else nc.scalar.copy, half, 0, raw[:])
+                    split = (H, H // 2, 0, 0, 0, 0)[step]
+                    if split > 0:
+                        round_rows(nc.vector.tensor_copy, half, 0, raw[:, :, 0:split])
+                    if split < H:
+                        round_rows(nc.scalar.copy, half, split, raw[:, :, split:H])
                     quantise(half, codes, scales, 0, H)
                 multiply_pass(e, o, banks, codes, scales)
                 if e > 0 and step == 3:
@@ -163,8 +180,6 @@ def tile_moe_res_glu_silu_kernel(
                     for st in range(SLOT_TILES):
                         nc.scalar.activation(acts[st], by_word(a_banks[st]), SILU)
             w2_raw = load_rows(w2[e])
-            if e == 0:
-                nc.sync.dma_start(gates[:], gate[0:P, :])
             if last:
                 for b in range(N_BLOCKS):
                     rows = raws.tile([P, T], F32, name="rows", tag="raw")
@@ -214,8 +229,8 @@ def tile_moe_res_glu_silu_kernel(
         for b in range(N_BLOCKS):
             y = results.tile([P, C], F32, name="y")
             scatter(E - 1, b, sums, y[:])
-            pieces = 2 if b == N_BLOCKS - 1 else 1
-            for piece in range(pieces):
-                cols = slice(piece * T // pieces, (piece + 1) * T // pieces)
+            edges = (0, 512, 1024, T) if b == N_BLOCKS - 1 else (0, T)
+            for c0, c1 in zip(edges, edges[1:]):
+                cols = slice(c0, c1)
                 nc.vector.tensor_tensor(residual[b][:, cols], residual[b][:, cols], windows[b][:, cols], ADD)
                 nc.sync.dma_start(out[b * P : (b + 1) * P, cols], residual[b][:, cols])

@@ -27,7 +27,7 @@ N_BLOCKS = N // P
 SLOT_TILES = C // P
 GATHER = 512
 PER_COL = 16
-RAW_BUFS = 10
+RAW_BUFS = 12
 
 
 def tile_moe_res_glu_silu_kernel(
@@ -156,26 +156,17 @@ def tile_moe_res_glu_silu_kernel(
                 weights, banks = ((w1, a_banks), (w3, b_banks))[step // PASSES]
                 rows = weights[e, o * K_PASS : (o + 1) * K_PASS, :]
                 half, codes, scales = operand_tiles(H)
-                if last and step == 2 * PASSES - 1:
-                    for copy, c0 in ((nc.scalar.copy, 0), (nc.vector.tensor_copy, H // 2)):
-                        raw = load_rows(rows[:, c0 : c0 + H // 2])
-                        round_rows(copy, half, c0, raw[:])
-                        quantise(half, codes, scales, c0, c0 + H // 2)
-                else:
-                    raw = head[o] if e == 0 and step < PASSES else load_rows(rows)
-                    split = (H, H // 2, 0, 0, 0, 0)[step]
-                    if split > 0:
-                        round_rows(nc.vector.tensor_copy, half, 0, raw[:, :, 0:split])
-                    if split < H:
-                        round_rows(nc.scalar.copy, half, split, raw[:, :, split:H])
-                    quantise(half, codes, scales, 0, H)
+                raw = head[o] if e == 0 and step < PASSES else load_rows(rows)
+                split = H // 2 if step in (3, 5) else 0
+                if split > 0:
+                    round_rows(nc.vector.tensor_copy, half, 0, raw[:, :, 0:split])
+                round_rows(nc.scalar.copy, half, split, raw[:, :, split:H])
+                quantise(half, codes, scales, 0, H)
                 multiply_pass(e, o, banks, codes, scales)
-                if e > 0 and step == 3:
-                    for b in range(N_BLOCKS - 1 if last else N_BLOCKS):
+                if e > 0:
+                    for b in {1: (0, 1), 2: (2,)}.get(step, ()):
                         scatter(e - 1, b, sums, raw[:, b, 0:C])
-                if last and step == 4:
-                    scatter(e - 1, N_BLOCKS - 1, sums, half[:, 0 : 2 * C].bitcast(F32))
-                if step == (4 if last else 5):
+                if step == 4:
                     acts = [raw[:, st, :].rearrange("s (u p r) -> s u p r", u=2, r=2) for st in range(SLOT_TILES)]
                     for st in range(SLOT_TILES):
                         nc.scalar.activation(acts[st], by_word(a_banks[st]), SILU)
@@ -204,11 +195,7 @@ def tile_moe_res_glu_silu_kernel(
             nc.vector.quantize_mx(out=h_codes[:].bitcast(FP8X4), scales=h_scales[:], in_=hidden_t[:])
 
             half, w2_codes, w2_scales = operand_tiles(N)
-            if last:
-                round_rows(nc.scalar.copy, half, 0, w2_raw[:])
-            else:
-                round_rows(nc.vector.tensor_copy, half, 0, w2_raw[:, :, 0 : N // 2])
-                round_rows(nc.scalar.copy, half, N // 2, w2_raw[:, :, N // 2 : N])
+            round_rows(nc.scalar.copy if last else nc.vector.tensor_copy, half, 0, w2_raw[:])
             quantise(half, w2_codes, w2_scales, 0, 256)
             quantise(half, w2_codes, w2_scales, 256, N)
             y_first = psum.tile([P, C], F32, name="y_first")
@@ -229,7 +216,7 @@ def tile_moe_res_glu_silu_kernel(
         for b in range(N_BLOCKS):
             y = results.tile([P, C], F32, name="y")
             scatter(E - 1, b, sums, y[:])
-            edges = (0, 512, 1024, T) if b == N_BLOCKS - 1 else (0, T)
+            edges = (0, T // 2, T) if b == N_BLOCKS - 1 else (0, T)
             for c0, c1 in zip(edges, edges[1:]):
                 cols = slice(c0, c1)
                 nc.vector.tensor_tensor(residual[b][:, cols], residual[b][:, cols], windows[b][:, cols], ADD)

@@ -23,11 +23,23 @@ P = 128
 PACK = 4
 K_PASS = P * PACK
 PASSES = K // K_PASS
+QUADRANT = 32
 N_BLOCKS = N // P
 SLOT_TILES = C // P
-GATHER = 512
 PER_COL = 16
+GATHER = 2 * C
+LINE = 4
+PER_BANK = 4
+W2_FIRST = 256
+
+STEPS = 2 * PASSES
+SHARED_STEPS = (PASSES, STEPS - 1)
+SCATTERS_BEHIND = {1: (0, 1), 2: (2,)}
+SILU_STEP = STEPS - 2
+
 RAW_BUFS = 12
+HALF_BUFS = 10
+CODE_BUFS = 8
 
 
 def tile_moe_res_glu_silu_kernel(
@@ -37,14 +49,13 @@ def tile_moe_res_glu_silu_kernel(
     with ExitStack() as ctx:
         keep = ctx.enter_context(tc.tile_pool(name="keep", bufs=1))
         raws = ctx.enter_context(tc.tile_pool(name="raws", bufs=RAW_BUFS))
-        halves = ctx.enter_context(tc.tile_pool(name="halves", bufs=10))
-        coded = ctx.enter_context(tc.tile_pool(name="coded", bufs=8))
+        halves = ctx.enter_context(tc.tile_pool(name="halves", bufs=HALF_BUFS))
+        coded = ctx.enter_context(tc.tile_pool(name="coded", bufs=CODE_BUFS))
         work = ctx.enter_context(tc.tile_pool(name="work", bufs=2))
-        results = ctx.enter_context(tc.tile_pool(name="results", bufs=3))
+        results = ctx.enter_context(tc.tile_pool(name="results", bufs=N_BLOCKS))
         psum = ctx.enter_context(tc.psum_pool(name="psum", bufs=1))
 
         offsets = keep.tile([P, S // PER_COL], U16, name="offsets")
-        nc.sync.dma_start(offsets[:], offs)
 
         token_scales = keep.tile([P, T], U8, name="token_scales", align_bytes=64)
         nc.vector.memset(token_scales[:].bitcast(I32), 0)
@@ -54,8 +65,6 @@ def tile_moe_res_glu_silu_kernel(
             nc.gpsimd.memset(window[:], 0.0)
         identity = keep.tile([P, P], F32, name="identity")
         make_identity(nc, identity[:])
-        warm = keep.tile([P, 1], F32, name="warm")
-        nc.scalar.activation(warm[:], windows[0][:, 0:1], SILU)
 
         token_words = [keep.tile([P, T], U32, name=f"token_words{o}", align_bytes=64) for o in range(PASSES)]
         slot_words = [keep.tile([P, S], U32, name=f"slot_words{o}", align_bytes=64) for o in range(PASSES)]
@@ -69,7 +78,7 @@ def tile_moe_res_glu_silu_kernel(
 
         def load_token_scales(q):
             nc.sync.dma_start(
-                token_scales[:].bitcast(I32)[32 * q : 32 * q + PACK * PASSES, :],
+                token_scales[:].bitcast(I32)[QUADRANT * q : QUADRANT * q + PACK * PASSES, :],
                 x_scales.bitcast(I32)[:, PACK * q : PACK * (q + 1), :],
             )
 
@@ -92,8 +101,8 @@ def tile_moe_res_glu_silu_kernel(
         def round_rows(copy, half, c0, raw):
             c1 = c0 + raw.shape[2]
             copy(
-                half[:, PACK * c0 : PACK * c1].rearrange("p (c i j) -> p c j i", i=4, j=PACK),
-                raw.rearrange("p j (c i) -> p c j i", i=4),
+                half[:, PACK * c0 : PACK * c1].rearrange("p (c i j) -> p c j i", i=LINE, j=PACK),
+                raw.rearrange("p j (c i) -> p c j i", i=LINE),
             )
 
         def quantise(half, codes, scales, c0, c1):
@@ -114,34 +123,41 @@ def tile_moe_res_glu_silu_kernel(
                     stop=(o == PASSES - 1),
                 )
 
-        def by_word(bank):
+        def bank_by_pairs(bank):
             return bank[:].rearrange("s (p u r) -> s u p r", u=2, r=2)
+
+        def as_pairs(row):
+            return row.rearrange("s (u p r) -> s u p r", u=2, r=2)
 
         def scatter(e, b, sums, y):
             listed = offsets[:, e * C // PER_COL : (e + 1) * C // PER_COL]
             nc.scalar.copy(y, sums[b])
             nc.vector.tensor_tensor(windows[b][:].indirect(listed), y, gates[:, e * C : (e + 1) * C], MULT)
 
+        load_tokens(0)
+        nc.sync.dma_start(offsets[:], offs)
+
         per_row = S // P
         gate_cols = keep.tile([P, per_row], F32, name="gate_cols")
         nc.sync.dma_start(gate_cols[:], gate[0:1, :].rearrange("o (p m) -> (o p) m", m=per_row))
-        for g in range(per_row // 4):
-            spread = psum.tile([P, 4, P], F32, name="spread", tag=f"a{g}")
-            for m in range(4):
-                column = gate_cols[:, 4 * g + m : 4 * g + m + 1].to_broadcast([P, P])
+        for g in range(per_row // PER_BANK):
+            spread = psum.tile([P, PER_BANK, P], F32, name="spread", tag=f"a{g}")
+            for m in range(PER_BANK):
+                column = gate_cols[:, PER_BANK * g + m : PER_BANK * g + m + 1].to_broadcast([P, P])
                 nc.tensor.transpose(spread[:, m, :], column, identity[:])
             nc.scalar.copy(
-                gates[:].rearrange("q (p m) -> q p m", m=per_row)[:, :, 4 * g : 4 * g + 4],
+                gates[:].rearrange("q (p m) -> q p m", m=per_row)[:, :, PER_BANK * g : PER_BANK * (g + 1)],
                 spread[:].rearrange("q m p -> q p m"),
             )
 
-        head = []
+        preloaded = []
         for o in range(PASSES):
-            load_tokens(o)
-            head.append(load_rows(w1[0, o * K_PASS : (o + 1) * K_PASS, :]))
+            if o > 0:
+                load_tokens(o)
+            preloaded.append(load_rows(w1[0, o * K_PASS : (o + 1) * K_PASS, :]))
             load_token_scales(o)
             if o == 0:
-                load_token_scales(PASSES)
+                load_token_scales(P // QUADRANT - 1)
 
         residual = []
         sums = None
@@ -151,25 +167,28 @@ def tile_moe_res_glu_silu_kernel(
                 gather(e * C)
             a_banks = [psum.tile([P, H], F32, name=f"a{st}", tag=f"a{st}") for st in range(SLOT_TILES)]
             b_banks = [psum.tile([P, H], F32, name=f"b{st}", tag=f"b{st}") for st in range(SLOT_TILES)]
-            for step in range(2 * PASSES):
+            for step in range(STEPS):
                 o = step % PASSES
                 weights, banks = ((w1, a_banks), (w3, b_banks))[step // PASSES]
-                rows = weights[e, o * K_PASS : (o + 1) * K_PASS, :]
                 half, codes, scales = operand_tiles(H)
-                raw = head[o] if e == 0 and step < PASSES else load_rows(rows)
-                split = H // 2 if step in (3, 5) else 0
+                if e == 0 and step < PASSES:
+                    raw = preloaded[o]
+                else:
+                    raw = load_rows(weights[e, o * K_PASS : (o + 1) * K_PASS, :])
+                split = H // 2 if step in SHARED_STEPS else 0
                 if split > 0:
                     round_rows(nc.vector.tensor_copy, half, 0, raw[:, :, 0:split])
+                    quantise(half, codes, scales, 0, split)
                 round_rows(nc.scalar.copy, half, split, raw[:, :, split:H])
-                quantise(half, codes, scales, 0, H)
+                quantise(half, codes, scales, split, H)
                 multiply_pass(e, o, banks, codes, scales)
                 if e > 0:
-                    for b in {1: (0, 1), 2: (2,)}.get(step, ()):
+                    for b in SCATTERS_BEHIND.get(step, ()):
                         scatter(e - 1, b, sums, raw[:, b, 0:C])
-                if step == 4:
-                    acts = [raw[:, st, :].rearrange("s (u p r) -> s u p r", u=2, r=2) for st in range(SLOT_TILES)]
+                if step == SILU_STEP:
+                    acts = [as_pairs(raw[:, st, :]) for st in range(SLOT_TILES)]
                     for st in range(SLOT_TILES):
-                        nc.scalar.activation(acts[st], by_word(a_banks[st]), SILU)
+                        nc.scalar.activation(acts[st], bank_by_pairs(a_banks[st]), SILU)
             w2_raw = load_rows(w2[e])
             if last:
                 for b in range(N_BLOCKS):
@@ -177,27 +196,26 @@ def tile_moe_res_glu_silu_kernel(
                     nc.sync.dma_start(rows[:], xr[b * P : (b + 1) * P, :])
                     residual.append(rows)
 
+            copy_late = nc.scalar.copy if last else nc.vector.tensor_copy
             hidden_t = work.tile([P, C * PACK], BF16, name="hidden_t", align_bytes=64)
+            h_codes = work.tile([P, C], U32, name="h_codes", align_bytes=64)
+            h_scales = work.tile([P, C], U8, name="h_scales", align_bytes=64)
             for st in range(SLOT_TILES):
                 hidden = work.tile([P, H], BF16, name="hidden", tag=f"hidden{st}")
-                nc.vector.tensor_tensor(
-                    hidden[:].rearrange("s (u p r) -> s u p r", u=2, r=2), by_word(b_banks[st]), acts[st], MULT
-                )
+                nc.vector.tensor_tensor(as_pairs(hidden[:]), bank_by_pairs(b_banks[st]), acts[st], MULT)
                 turned = psum.tile([P, 2, P], F32, name="turned", tag=f"turned{st}")
                 for u in range(2):
                     nc.tensor.transpose(turned[:, u, :], hidden[:].bitcast(F32)[:, u * P : (u + 1) * P], identity[:])
-                (nc.scalar.copy if last else nc.vector.tensor_copy)(
+                copy_late(
                     hidden_t[:].bitcast(F32)[:, st * 2 * P : (st + 1) * 2 * P].rearrange("p (s u) -> p s u", u=2),
                     turned[:].rearrange("p u s -> p s u"),
                 )
-            h_codes = work.tile([P, C], U32, name="h_codes", align_bytes=64)
-            h_scales = work.tile([P, C], U8, name="h_scales", align_bytes=64)
-            nc.vector.quantize_mx(out=h_codes[:].bitcast(FP8X4), scales=h_scales[:], in_=hidden_t[:])
+                quantise(hidden_t, h_codes, h_scales, st * P, (st + 1) * P)
 
             half, w2_codes, w2_scales = operand_tiles(N)
-            round_rows(nc.scalar.copy if last else nc.vector.tensor_copy, half, 0, w2_raw[:])
-            quantise(half, w2_codes, w2_scales, 0, 256)
-            quantise(half, w2_codes, w2_scales, 256, N)
+            round_rows(copy_late, half, 0, w2_raw[:])
+            quantise(half, w2_codes, w2_scales, 0, W2_FIRST)
+            quantise(half, w2_codes, w2_scales, W2_FIRST, N)
             y_first = psum.tile([P, C], F32, name="y_first")
             y_rest = psum.tile([P, N_BLOCKS - 1, C], F32, name="y_rest")
             sums = [y_first[:]] + [y_rest[:, b, :] for b in range(N_BLOCKS - 1)]
@@ -213,11 +231,35 @@ def tile_moe_res_glu_silu_kernel(
                     stop=True,
                 )
 
-        for b in range(N_BLOCKS):
-            y = results.tile([P, C], F32, name="y")
-            scatter(E - 1, b, sums, y[:])
-            edges = (0, T // 2, T) if b == N_BLOCKS - 1 else (0, T)
-            for c0, c1 in zip(edges, edges[1:]):
-                cols = slice(c0, c1)
+        def add_residual_by_transposes(b):
+            for g, (there, back) in enumerate((("a0", "b1"), ("a1", "turned0"), ("b0", "turned1"))):
+                c0 = g * PER_BANK * P
+                blocks = min(PER_BANK, (T - c0) // P)
+                by_token = psum.tile([P, blocks, P], F32, name="by_token", tag=there)
+                for m in range(blocks):
+                    cols = slice(c0 + m * P, c0 + (m + 1) * P)
+                    for part, first in ((residual[b], True), (windows[b], False)):
+                        nc.tensor.matmul(
+                            by_token[:, m, :], part[:, cols], identity[:], start=first, stop=not first, is_transpose=True
+                        )
+                summed = results.tile([P, blocks, P], F32, name="summed")
+                nc.scalar.copy(summed[:], by_token[:])
+                by_row = psum.tile([P, blocks, P], F32, name="by_row", tag=back)
+                for m in range(blocks):
+                    nc.tensor.transpose(by_row[:, m, :], summed[:, m, :], identity[:])
+                staged = results.tile([P, blocks * P], F32, name="staged")
+                nc.scalar.copy(staged[:], by_row[:].rearrange("n m t -> n (m t)"))
+                nc.scalar.dma_start(out[b * P : (b + 1) * P, c0 : c0 + blocks * P], staged[:])
+
+        def add_residual_on_vector(b, pieces):
+            for piece in range(pieces):
+                cols = slice(piece * T // pieces, (piece + 1) * T // pieces)
                 nc.vector.tensor_tensor(residual[b][:, cols], residual[b][:, cols], windows[b][:, cols], ADD)
                 nc.sync.dma_start(out[b * P : (b + 1) * P, cols], residual[b][:, cols])
+
+        scatter(E - 1, 0, sums, results.tile([P, C], F32, name="y")[:])
+        add_residual_by_transposes(0)
+        scatter(E - 1, 1, sums, results.tile([P, C], F32, name="y")[:])
+        add_residual_on_vector(1, pieces=1)
+        scatter(E - 1, 2, sums, residual[0][:, 0:C])
+        add_residual_on_vector(2, pieces=2)

from contextlib import ExitStack

import concourse.mybir as mybir
from concourse.masks import make_identity

K, T, E, C, H, N = 1536, 1280, 4, 256, 512, 384
S = E * C
FLOPS = 2 * S * (2 * K * H + H * N)
BYTES = K * T + K * T // 32 + 4 * (2 * N * T + E * (2 * K * H + H * N) + S) + 2 * 8 * S

F32 = mybir.dt.float32
BF16 = mybir.dt.bfloat16
I32 = mybir.dt.int32
U32 = mybir.dt.uint32
U16 = mybir.dt.uint16
U8 = mybir.dt.uint8
FP8X4 = mybir.dt.float8_e4m3fn_x4
MULT = mybir.AluOpType.mult
ADD = mybir.AluOpType.add
SILU = mybir.ActivationFunctionType.Silu

P = 128
PACK = 4
K_PASS = P * PACK
PASSES = K // K_PASS
QUADRANT = 32
N_BLOCKS = N // P
SLOT_TILES = C // P
PER_COL = 16
GATHER = 2 * C
LINE = 4
PER_BANK = 4
W2_FIRST = 256

STEPS = 2 * PASSES
SHARED_STEPS = (PASSES, STEPS - 1)
SCATTERS_BEHIND = {1: (0, 1), 2: (2,)}
SILU_STEP = STEPS - 2

RAW_BUFS = 12
HALF_BUFS = 10
CODE_BUFS = 8


def tile_moe_res_glu_silu_kernel(
    tc, x_words, x_scales, xr, w1, w3, w2, gate, offs, out
):
    nc = tc.nc
    with ExitStack() as ctx:
        keep = ctx.enter_context(tc.tile_pool(name="keep", bufs=1))
        raws = ctx.enter_context(tc.tile_pool(name="raws", bufs=RAW_BUFS))
        halves = ctx.enter_context(tc.tile_pool(name="halves", bufs=HALF_BUFS))
        coded = ctx.enter_context(tc.tile_pool(name="coded", bufs=CODE_BUFS))
        work = ctx.enter_context(tc.tile_pool(name="work", bufs=2))
        results = ctx.enter_context(tc.tile_pool(name="results", bufs=N_BLOCKS))
        psum = ctx.enter_context(tc.psum_pool(name="psum", bufs=1))

        offsets = keep.tile([P, S // PER_COL], U16, name="offsets")

        token_scales = keep.tile([P, T], U8, name="token_scales", align_bytes=64)
        nc.vector.memset(token_scales[:].bitcast(I32), 0)
        windows = [keep.tile([P, T], F32, name=f"window{b}") for b in range(N_BLOCKS)]
        nc.vector.memset(windows[0][:], 0.0)
        for window in windows[1:]:
            nc.gpsimd.memset(window[:], 0.0)
        identity = keep.tile([P, P], F32, name="identity")
        make_identity(nc, identity[:])

        token_words = [keep.tile([P, T], U32, name=f"token_words{o}", align_bytes=64) for o in range(PASSES)]
        slot_words = [keep.tile([P, S], U32, name=f"slot_words{o}", align_bytes=64) for o in range(PASSES)]
        slot_scales = keep.tile([P, S], U8, name="slot_scales", align_bytes=64)
        gates = keep.tile([P, S], F32, name="gates")

        def load_tokens(o):
            nc.sync.dma_start(
                token_words[o][:].bitcast(I32), x_words[o].rearrange("p t r -> p (t r)").bitcast(I32)
            )

        def load_token_scales(q):
            nc.sync.dma_start(
                token_scales[:].bitcast(I32)[QUADRANT * q : QUADRANT * q + PACK * PASSES, :],
                x_scales.bitcast(I32)[:, PACK * q : PACK * (q + 1), :],
            )

        def gather(s0):
            listed = offsets[:, s0 // PER_COL : (s0 + GATHER) // PER_COL]
            for dst, src in list(zip(slot_words, token_words)) + [(slot_scales, token_scales)]:
                nc.vector.tensor_copy(dst[:, s0 : s0 + GATHER], src[:].indirect(listed))

        def load_rows(rows):
            raw = raws.tile([P, PACK, rows.shape[1]], F32, name="raw", tag="raw")
            nc.sync.dma_start(raw[:], rows.rearrange("(p j) w -> p j w", j=PACK))
            return raw

        def operand_tiles(width):
            half = halves.tile([P, PACK * width], BF16, name="half", tag="half", align_bytes=64)
            codes = coded.tile([P, width], U32, name="codes", tag="codes", align_bytes=64)
            scales = coded.tile([P, width], U8, name="scales", tag="scales", align_bytes=64)
            return half, codes, scales

        def round_rows(copy, half, c0, raw):
            c1 = c0 + raw.shape[2]
            copy(
                half[:, PACK * c0 : PACK * c1].rearrange("p (c i j) -> p c j i", i=LINE, j=PACK),
                raw.rearrange("p j (c i) -> p c j i", i=LINE),
            )

        def quantise(half, codes, scales, c0, c1):
            nc.vector.quantize_mx(
                out=codes[:, c0:c1].bitcast(FP8X4), scales=scales[:, c0:c1], in_=half[:, PACK * c0 : PACK * c1]
            )

        def multiply_pass(e, o, banks, codes, scales):
            for st in range(SLOT_TILES):
                slots = slice(e * C + st * P, e * C + (st + 1) * P)
                nc.tensor.matmul_mx(
                    out=banks[st][:],
                    lhsT=slot_words[o][:, slots].bitcast(FP8X4),
                    lhsT_scale=slot_scales[PACK * o : P, slots],
                    rhs=codes[:].bitcast(FP8X4),
                    rhs_scale=scales[:],
                    start=(o == 0),
                    stop=(o == PASSES - 1),
                )

        def bank_by_pairs(bank):
            return bank[:].rearrange("s (p u r) -> s u p r", u=2, r=2)

        def as_pairs(row):
            return row.rearrange("s (u p r) -> s u p r", u=2, r=2)

        def scatter(e, b, sums, y):
            listed = offsets[:, e * C // PER_COL : (e + 1) * C // PER_COL]
            nc.scalar.copy(y, sums[b])
            nc.vector.tensor_tensor(windows[b][:].indirect(listed), y, gates[:, e * C : (e + 1) * C], MULT)

        load_tokens(0)
        nc.sync.dma_start(offsets[:], offs)

        per_row = S // P
        gate_cols = keep.tile([P, per_row], F32, name="gate_cols")
        nc.sync.dma_start(gate_cols[:], gate[0:1, :].rearrange("o (p m) -> (o p) m", m=per_row))
        for g in range(per_row // PER_BANK):
            spread = psum.tile([P, PER_BANK, P], F32, name="spread", tag=f"a{g}")
            for m in range(PER_BANK):
                column = gate_cols[:, PER_BANK * g + m : PER_BANK * g + m + 1].to_broadcast([P, P])
                nc.tensor.transpose(spread[:, m, :], column, identity[:])
            nc.scalar.copy(
                gates[:].rearrange("q (p m) -> q p m", m=per_row)[:, :, PER_BANK * g : PER_BANK * (g + 1)],
                spread[:].rearrange("q m p -> q p m"),
            )

        preloaded = []
        for o in range(PASSES):
            if o > 0:
                load_tokens(o)
            preloaded.append(load_rows(w1[0, o * K_PASS : (o + 1) * K_PASS, :]))
            load_token_scales(o)
            if o == 0:
                load_token_scales(P // QUADRANT - 1)

        residual = []
        sums = None
        for e in range(E):
            last = e == E - 1
            if e * C % GATHER == 0:
                gather(e * C)
            a_banks = [psum.tile([P, H], F32, name=f"a{st}", tag=f"a{st}") for st in range(SLOT_TILES)]
            b_banks = [psum.tile([P, H], F32, name=f"b{st}", tag=f"b{st}") for st in range(SLOT_TILES)]
            for step in range(STEPS):
                o = step % PASSES
                weights, banks = ((w1, a_banks), (w3, b_banks))[step // PASSES]
                half, codes, scales = operand_tiles(H)
                if e == 0 and step < PASSES:
                    raw = preloaded[o]
                else:
                    raw = load_rows(weights[e, o * K_PASS : (o + 1) * K_PASS, :])
                split = H // 2 if step in SHARED_STEPS else 0
                if split > 0:
                    round_rows(nc.vector.tensor_copy, half, 0, raw[:, :, 0:split])
                    quantise(half, codes, scales, 0, split)
                round_rows(nc.scalar.copy, half, split, raw[:, :, split:H])
                quantise(half, codes, scales, split, H)
                multiply_pass(e, o, banks, codes, scales)
                if e > 0:
                    for b in SCATTERS_BEHIND.get(step, ()):
                        scatter(e - 1, b, sums, raw[:, b, 0:C])
                if step == SILU_STEP:
                    acts = [as_pairs(raw[:, st, :]) for st in range(SLOT_TILES)]
                    for st in range(SLOT_TILES):
                        nc.scalar.activation(acts[st], bank_by_pairs(a_banks[st]), SILU)
            w2_raw = load_rows(w2[e])
            if last:
                for b in range(N_BLOCKS):
                    rows = raws.tile([P, T], F32, name="rows", tag="raw")
                    nc.sync.dma_start(rows[:], xr[b * P : (b + 1) * P, :])
                    residual.append(rows)

            copy_late = nc.scalar.copy if last else nc.vector.tensor_copy
            hidden_t = work.tile([P, C * PACK], BF16, name="hidden_t", align_bytes=64)
            h_codes = work.tile([P, C], U32, name="h_codes", align_bytes=64)
            h_scales = work.tile([P, C], U8, name="h_scales", align_bytes=64)
            for st in range(SLOT_TILES):
                hidden = work.tile([P, H], BF16, name="hidden", tag=f"hidden{st}")
                nc.vector.tensor_tensor(as_pairs(hidden[:]), bank_by_pairs(b_banks[st]), acts[st], MULT)
                turned = psum.tile([P, 2, P], F32, name="turned", tag=f"turned{st}")
                for u in range(2):
                    nc.tensor.transpose(turned[:, u, :], hidden[:].bitcast(F32)[:, u * P : (u + 1) * P], identity[:])
                copy_late(
                    hidden_t[:].bitcast(F32)[:, st * 2 * P : (st + 1) * 2 * P].rearrange("p (s u) -> p s u", u=2),
                    turned[:].rearrange("p u s -> p s u"),
                )
                quantise(hidden_t, h_codes, h_scales, st * P, (st + 1) * P)

            half, w2_codes, w2_scales = operand_tiles(N)
            round_rows(copy_late, half, 0, w2_raw[:])
            quantise(half, w2_codes, w2_scales, 0, W2_FIRST)
            quantise(half, w2_codes, w2_scales, W2_FIRST, N)
            y_first = psum.tile([P, C], F32, name="y_first")
            y_rest = psum.tile([P, N_BLOCKS - 1, C], F32, name="y_rest")
            sums = [y_first[:]] + [y_rest[:, b, :] for b in range(N_BLOCKS - 1)]
            for b in range(N_BLOCKS):
                cols = slice(b * P, (b + 1) * P)
                nc.tensor.matmul_mx(
                    out=sums[b],
                    lhsT=w2_codes[:, cols].bitcast(FP8X4),
                    lhsT_scale=w2_scales[:, cols],
                    rhs=h_codes[:].bitcast(FP8X4),
                    rhs_scale=h_scales[:],
                    start=True,
                    stop=True,
                )

        def add_residual_by_transposes(b):
            for g, (there, back) in enumerate((("a0", "b1"), ("a1", "turned0"), ("b0", "turned1"))):
                c0 = g * PER_BANK * P
                blocks = min(PER_BANK, (T - c0) // P)
                by_token = psum.tile([P, blocks, P], F32, name="by_token", tag=there)
                for m in range(blocks):
                    cols = slice(c0 + m * P, c0 + (m + 1) * P)
                    for part, first in ((residual[b], True), (windows[b], False)):
                        nc.tensor.matmul(
                            by_token[:, m, :], part[:, cols], identity[:], start=first, stop=not first, is_transpose=True
                        )
                summed = results.tile([P, blocks, P], F32, name="summed")
                nc.scalar.copy(summed[:], by_token[:])
                by_row = psum.tile([P, blocks, P], F32, name="by_row", tag=back)
                for m in range(blocks):
                    nc.tensor.transpose(by_row[:, m, :], summed[:, m, :], identity[:])
                staged = results.tile([P, blocks * P], F32, name="staged")
                nc.scalar.copy(staged[:], by_row[:].rearrange("n m t -> n (m t)"))
                nc.scalar.dma_start(out[b * P : (b + 1) * P, c0 : c0 + blocks * P], staged[:])

        def add_residual_on_vector(b, pieces):
            for piece in range(pieces):
                cols = slice(piece * T // pieces, (piece + 1) * T // pieces)
                nc.vector.tensor_tensor(residual[b][:, cols], residual[b][:, cols], windows[b][:, cols], ADD)
                nc.sync.dma_start(out[b * P : (b + 1) * P, cols], residual[b][:, cols])

        scatter(E - 1, 0, sums, results.tile([P, C], F32, name="y")[:])
        add_residual_by_transposes(0)
        scatter(E - 1, 1, sums, results.tile([P, C], F32, name="y")[:])
        add_residual_on_vector(1, pieces=1)
        scatter(E - 1, 2, sums, residual[0][:, 0:C])
        add_residual_on_vector(2, pieces=2)
